import numpy as np
import ml_dtypes

BF16 = ml_dtypes.bfloat16


def bf(x):
    return np.asarray(x, np.float32).astype(BF16)


def f32(x):
    return np.asarray(x, np.float32)


def f64(x):
    return np.asarray(x).astype(np.float64)


def striped(idx):
    return np.tile(idx.reshape(-1, 16).T, (8, 1))


S, K, M, N, E, Q = 512, 128, 512, 384, 4, 96


def setup_inputs():
    return {"base": bf(np.random.standard_normal((M, S))), "x": bf(np.random.standard_normal((K, N))), "w": bf(np.random.standard_normal((E, K, M)) / np.sqrt(K)), "b": f32(0.5 * np.random.standard_normal((M, 1))), "offs": striped(np.random.permutation(S)[:N])}


def reference(base, x, w, b, offs):
    idx = offs[:16].T.reshape(-1)
    z = f64(base).copy()
    for e in range(E):
        z[:, idx[e * Q : (e + 1) * Q]] += f64(w)[e].T @ f64(x)[:, e * Q : (e + 1) * Q]
    return np.maximum(z + f64(b), 0.0)

@@ -1,0 +1,74 @@
+import concourse.mybir as mybir
+from concourse.masks import make_identity
+
+P = 128
+S = 512
+M = 512
+N = 384
+E = 4
+Q = N // E
+BLOCKS = M // P
+QCOLS = Q // 16
+
+FLOPS = 2 * P * M * N
+
+BF16 = mybir.dt.bfloat16
+F32 = mybir.dt.float32
+U16 = mybir.dt.uint16
+
+
+def tile_scatter_matmul_kernel(tc, base, x, w, b, offs, out):
+    nc = tc.nc
+    relu = mybir.ActivationFunctionType.Relu
+    add, vmax = mybir.AluOpType.add, mybir.AluOpType.max
+
+    with (
+        tc.tile_pool(name="held", bufs=1) as held,
+        tc.psum_pool(name="banks", bufs=1) as banks,
+    ):
+        offsets = held.tile([P, N // 16], U16, name="offsets")
+        nc.sync.dma_start(offsets[:], offs)
+
+        ident = held.tile([P, P], BF16, name="ident")
+        make_identity(nc, ident[:])
+
+        base_tiles = []
+        for a in range(BLOCKS):
+            base_tile = held.tile([P, S], BF16, name="base%d" % a)
+            nc.sync.dma_start(base_tile[:], base[a * P : (a + 1) * P, :])
+            base_tiles.append(base_tile)
+
+        x_tile = held.tile([P, N], BF16, name="x_tile")
+        nc.scalar.dma_start(x_tile[:], x)
+        w_tiles = []
+        for e in range(E):
+            w_tile = held.tile([P, M], BF16, name="w%d" % e)
+            nc.scalar.dma_start(w_tile[:], w[e])
+            w_tiles.append(w_tile)
+
+        bias = held.tile([P, BLOCKS], F32, name="bias")
+        with nc.allow_non_contiguous_dma(reason="one float32 to a partition"):
+            nc.gpsimd.dma_start(bias[:], b.rearrange("(a p) o -> p (a o)", p=P))
+
+        windows = []
+        for a in range(BLOCKS):
+            window = banks.tile([P, S], F32, name="window%d" % a)
+            nc.tensor.matmul(window[:], ident[:], base_tiles[a][:], start=True, stop=False)
+            windows.append(window)
+
+        for a in range(BLOCKS):
+            for e in range(E):
+                nc.tensor.matmul(
+                    windows[a][:].indirect(offsets[:, e * QCOLS : (e + 1) * QCOLS]),
+                    w_tiles[e][:, a * P : (a + 1) * P],
+                    x_tile[:, e * Q : (e + 1) * Q],
+                    start=False,
+                    stop=(e == E - 1),
+                )
+
+            result = held.tile([P, S], F32, name="result%d" % a)
+            if a % 2 == 0:
+                nc.scalar.activation(result[:], windows[a][:], relu, bias=bias[:, a : a + 1])
+            else:
+                nc.vector.tensor_scalar(result[:], windows[a][:], bias[:, a : a + 1], 0.0, add, vmax)
+            nc.sync.dma_start(out[a * P : (a + 1) * P, :], result[:])

@@ -9,6 +9,8 @@ E = 4
 Q = N // E
 BLOCKS = M // P
 QCOLS = Q // 16
+HALF = M // 2
+WARM = 3
 
 FLOPS = 2 * P * M * N
 
@@ -26,29 +28,34 @@ def tile_scatter_matmul_kernel(tc, base, x, w, b, offs, out):
         tc.tile_pool(name="held", bufs=1) as held,
         tc.psum_pool(name="banks", bufs=1) as banks,
     ):
-        offsets = held.tile([P, N // 16], U16, name="offsets")
-        nc.sync.dma_start(offsets[:], offs)
+        zeros_f32 = held.tile([P, S // 2], F32, name="zeros_f32")
+        nc.vector.memset(zeros_f32[:], 0.0)
+        zeros = zeros_f32[:].bitcast(BF16)
+        warm_bank = banks.tile([P, S], F32, name="warm_bank")
+        for i in range(WARM):
+            nc.tensor.matmul(warm_bank[:], zeros[:, 0:P], zeros, start=True, stop=True)
 
         ident = held.tile([P, P], BF16, name="ident")
         make_identity(nc, ident[:])
+
+        bias = held.tile([P, BLOCKS], F32, name="bias")
+        with nc.allow_non_contiguous_dma(reason="one float32 to a partition"):
+            nc.scalar.dma_start(bias[:], b.rearrange("(a p) o -> p (a o)", p=P))
+        x_tile = held.tile([P, N], BF16, name="x_tile")
+        nc.scalar.dma_start(x_tile[:], x)
 
         base_tiles = []
         for a in range(BLOCKS):
             base_tile = held.tile([P, S], BF16, name="base%d" % a)
             nc.sync.dma_start(base_tile[:], base[a * P : (a + 1) * P, :])
             base_tiles.append(base_tile)
-
-        x_tile = held.tile([P, N], BF16, name="x_tile")
-        nc.scalar.dma_start(x_tile[:], x)
-        w_tiles = []
-        for e in range(E):
-            w_tile = held.tile([P, M], BF16, name="w%d" % e)
-            nc.scalar.dma_start(w_tile[:], w[e])
-            w_tiles.append(w_tile)
-
-        bias = held.tile([P, BLOCKS], F32, name="bias")
-        with nc.allow_non_contiguous_dma(reason="one float32 to a partition"):
-            nc.gpsimd.dma_start(bias[:], b.rearrange("(a p) o -> p (a o)", p=P))
+        offsets = held.tile([P, N // 16], U16, name="offsets")
+        nc.sync.dma_start(offsets[:], offs)
+        w_halves = []
+        for h in range(M // HALF):
+            w_half = held.tile([P, E, HALF], BF16, name="w_half%d" % h)
+            nc.sync.dma_start(w_half[:], w[:, :, h * HALF : (h + 1) * HALF].rearrange("e k m -> k e m"))
+            w_halves.append(w_half)
 
         windows = []
         for a in range(BLOCKS):
@@ -60,7 +67,7 @@ def tile_scatter_matmul_kernel(tc, base, x, w, b, offs, out):
             for e in range(E):
                 nc.tensor.matmul(
                     windows[a][:].indirect(offsets[:, e * QCOLS : (e + 1) * QCOLS]),
-                    w_tiles[e][:, a * P : (a + 1) * P],
+                    w_halves[a * P // HALF][:, e, a * P % HALF : a * P % HALF + P],
                     x_tile[:, e * Q : (e + 1) * Q],
                     start=False,
                     stop=(e == E - 1),

@@ -75,7 +75,8 @@ def tile_scatter_matmul_kernel(tc, base, x, w, b, offs, out):
 
             result = held.tile([P, S], F32, name="result%d" % a)
             if a % 2 == 0:
-                nc.scalar.activation(result[:], windows[a][:], relu, bias=bias[:, a : a + 1])
-            else:
                 nc.vector.tensor_scalar(result[:], windows[a][:], bias[:, a : a + 1], 0.0, add, vmax)
-            nc.sync.dma_start(out[a * P : (a + 1) * P, :], result[:])
+                nc.sync.dma_start(out[a * P : (a + 1) * P, :], result[:])
+            else:
+                nc.scalar.activation(result[:], windows[a][:], relu, bias=bias[:, a : a + 1])
+                nc.scalar.dma_start(out[a * P : (a + 1) * P, :], result[:])

@@ -35,14 +35,20 @@ def tile_scatter_matmul_kernel(tc, base, x, w, b, offs, out):
         for i in range(WARM):
             nc.tensor.matmul(warm_bank[:], zeros[:, 0:P], zeros, start=True, stop=True)
 
+        b_rows = held.tile([P, P], F32, name="b_rows")
+        nc.gpsimd.memset(b_rows[:], 0.0)
+
         ident = held.tile([P, P], BF16, name="ident")
         make_identity(nc, ident[:])
+        ident_f32 = held.tile([P, P], F32, name="ident_f32")
+        make_identity(nc, ident_f32[:])
 
-        bias = held.tile([P, BLOCKS], F32, name="bias")
-        with nc.allow_non_contiguous_dma(reason="one float32 to a partition"):
-            nc.scalar.dma_start(bias[:], b.rearrange("(a p) o -> p (a o)", p=P))
         x_tile = held.tile([P, N], BF16, name="x_tile")
         nc.scalar.dma_start(x_tile[:], x)
+        nc.scalar.dma_start(b_rows[0:BLOCKS, :], b.rearrange("(a p) o -> a (p o)", p=P))
+
+        early_relu = held.tile([P, 1], F32, name="early_relu")
+        nc.scalar.activation(early_relu[:], zeros_f32[:, 0:1], relu)
 
         base_tiles = []
         for a in range(BLOCKS):
@@ -62,6 +68,11 @@ def tile_scatter_matmul_kernel(tc, base, x, w, b, offs, out):
             window = banks.tile([P, S], F32, name="window%d" % a)
             nc.tensor.matmul(window[:], ident[:], base_tiles[a][:], start=True, stop=False)
             windows.append(window)
+
+        bias_bank = banks.tile([P, P], F32, name="bias_bank")
+        nc.tensor.transpose(bias_bank[:], b_rows[:], ident_f32[:])
+        bias = held.tile([P, BLOCKS], F32, name="bias")
+        nc.vector.tensor_copy(bias[:], bias_bank[:, 0:BLOCKS])
 
         for a in range(BLOCKS):
             for e in range(E):

@@ -9,7 +9,6 @@ E = 4
 Q = N // E
 BLOCKS = M // P
 QCOLS = Q // 16
-HALF = M // 2
 WARM = 3
 
 FLOPS = 2 * P * M * N
@@ -43,8 +42,6 @@ def tile_scatter_matmul_kernel(tc, base, x, w, b, offs, out):
         ident_f32 = held.tile([P, P], F32, name="ident_f32")
         make_identity(nc, ident_f32[:])
 
-        x_tile = held.tile([P, N], BF16, name="x_tile")
-        nc.scalar.dma_start(x_tile[:], x)
         nc.scalar.dma_start(b_rows[0:BLOCKS, :], b.rearrange("(a p) o -> a (p o)", p=P))
 
         early_relu = held.tile([P, 1], F32, name="early_relu")
@@ -55,13 +52,15 @@ def tile_scatter_matmul_kernel(tc, base, x, w, b, offs, out):
             base_tile = held.tile([P, S], BF16, name="base%d" % a)
             nc.sync.dma_start(base_tile[:], base[a * P : (a + 1) * P, :])
             base_tiles.append(base_tile)
+        x_tile = held.tile([P, N], BF16, name="x_tile")
+        nc.sync.dma_start(x_tile[:], x)
         offsets = held.tile([P, N // 16], U16, name="offsets")
         nc.sync.dma_start(offsets[:], offs)
-        w_halves = []
-        for h in range(M // HALF):
-            w_half = held.tile([P, E, HALF], BF16, name="w_half%d" % h)
-            nc.sync.dma_start(w_half[:], w[:, :, h * HALF : (h + 1) * HALF].rearrange("e k m -> k e m"))
-            w_halves.append(w_half)
+        w_tiles = []
+        for a in range(BLOCKS):
+            w_tile = held.tile([P, E, P], BF16, name="w%d" % a)
+            nc.sync.dma_start(w_tile[:], w[:, :, a * P : (a + 1) * P].rearrange("e k m -> k e m"))
+            w_tiles.append(w_tile)
 
         windows = []
         for a in range(BLOCKS):
@@ -78,7 +77,7 @@ def tile_scatter_matmul_kernel(tc, base, x, w, b, offs, out):
             for e in range(E):
                 nc.tensor.matmul(
                     windows[a][:].indirect(offsets[:, e * QCOLS : (e + 1) * QCOLS]),
-                    w_halves[a * P // HALF][:, e, a * P % HALF : a * P % HALF + P],
+                    w_tiles[a][:, e, :],
                     x_tile[:, e * Q : (e + 1) * Q],
                     start=False,
                     stop=(e == E - 1),

@@ -9,6 +9,7 @@ E = 4
 Q = N // E
 BLOCKS = M // P
 QCOLS = Q // 16
+LINE = 256
 WARM = 3
 
 FLOPS = 2 * P * M * N
@@ -49,16 +50,16 @@ def tile_scatter_matmul_kernel(tc, base, x, w, b, offs, out):
 
         base_tiles = []
         for a in range(BLOCKS):
-            base_tile = held.tile([P, S], BF16, name="base%d" % a)
+            base_tile = held.tile([P, S], BF16, name="base%d" % a, align_bytes=LINE)
             nc.sync.dma_start(base_tile[:], base[a * P : (a + 1) * P, :])
             base_tiles.append(base_tile)
-        x_tile = held.tile([P, N], BF16, name="x_tile")
+        x_tile = held.tile([P, N], BF16, name="x_tile", align_bytes=LINE)
         nc.sync.dma_start(x_tile[:], x)
         offsets = held.tile([P, N // 16], U16, name="offsets")
         nc.sync.dma_start(offsets[:], offs)
         w_tiles = []
         for a in range(BLOCKS):
-            w_tile = held.tile([P, E, P], BF16, name="w%d" % a)
+            w_tile = held.tile([P, E, P], BF16, name="w%d" % a, align_bytes=LINE)
             nc.sync.dma_start(w_tile[:], w[:, :, a * P : (a + 1) * P].rearrange("e k m -> k e m"))
             w_tiles.append(w_tile)
 
@@ -83,7 +84,7 @@ def tile_scatter_matmul_kernel(tc, base, x, w, b, offs, out):
                     stop=(e == E - 1),
                 )
 
-            result = held.tile([P, S], F32, name="result%d" % a)
+            result = held.tile([P, S], F32, name="result%d" % a, align_bytes=LINE)
             if a % 2 == 0:
                 nc.vector.tensor_scalar(result[:], windows[a][:], bias[:, a : a + 1], 0.0, add, vmax)
                 nc.sync.dma_start(out[a * P : (a + 1) * P, :], result[:])

@@ -10,7 +10,7 @@ Q = N // E
 BLOCKS = M // P
 QCOLS = Q // 16
 LINE = 256
-WARM = 3
+WARM = 14
 
 FLOPS = 2 * P * M * N
 
@@ -28,12 +28,12 @@ def tile_scatter_matmul_kernel(tc, base, x, w, b, offs, out):
         tc.tile_pool(name="held", bufs=1) as held,
         tc.psum_pool(name="banks", bufs=1) as banks,
     ):
-        zeros_f32 = held.tile([P, S // 2], F32, name="zeros_f32")
-        nc.vector.memset(zeros_f32[:], 0.0)
+        zeros_f32 = held.tile([P, P // 2], F32, name="zeros_f32")
+        nc.gpsimd.memset(zeros_f32[:], 0.0)
         zeros = zeros_f32[:].bitcast(BF16)
-        warm_bank = banks.tile([P, S], F32, name="warm_bank")
+        warm_bank = banks.tile([P, P], F32, name="warm_bank")
         for i in range(WARM):
-            nc.tensor.matmul(warm_bank[:], zeros[:, 0:P], zeros, start=True, stop=True)
+            nc.tensor.matmul(warm_bank[:], zeros, zeros, start=True, stop=True)
 
         b_rows = held.tile([P, P], F32, name="b_rows")
         nc.gpsimd.memset(b_rows[:], 0.0)

@@ -85,7 +85,7 @@ def tile_scatter_matmul_kernel(tc, base, x, w, b, offs, out):
                 )
 
             result = held.tile([P, S], F32, name="result%d" % a, align_bytes=LINE)
-            if a % 2 == 0:
+            if a < BLOCKS // 2:
                 nc.vector.tensor_scalar(result[:], windows[a][:], bias[:, a : a + 1], 0.0, add, vmax)
                 nc.sync.dma_start(out[a * P : (a + 1) * P, :], result[:])
             else:

@@ -85,9 +85,9 @@ def tile_scatter_matmul_kernel(tc, base, x, w, b, offs, out):
                 )
 
             result = held.tile([P, S], F32, name="result%d" % a, align_bytes=LINE)
-            if a < BLOCKS // 2:
+            if a == 1:
                 nc.vector.tensor_scalar(result[:], windows[a][:], bias[:, a : a + 1], 0.0, add, vmax)
-                nc.sync.dma_start(out[a * P : (a + 1) * P, :], result[:])
             else:
                 nc.scalar.activation(result[:], windows[a][:], relu, bias=bias[:, a : a + 1])
-                nc.scalar.dma_start(out[a * P : (a + 1) * P, :], result[:])
+            store_queue = nc.sync if a < BLOCKS // 2 else nc.scalar
+            store_queue.dma_start(out[a * P : (a + 1) * P, :], result[:])

@@ -85,9 +85,9 @@ def tile_scatter_matmul_kernel(tc, base, x, w, b, offs, out):
                 )
 
             result = held.tile([P, S], F32, name="result%d" % a, align_bytes=LINE)
-            if a == 1:
-                nc.vector.tensor_scalar(result[:], windows[a][:], bias[:, a : a + 1], 0.0, add, vmax)
-            else:
+            if a % 2 == 0:
                 nc.scalar.activation(result[:], windows[a][:], relu, bias=bias[:, a : a + 1])
+            else:
+                nc.vector.tensor_scalar(result[:], windows[a][:], bias[:, a : a + 1], 0.0, add, vmax)
             store_queue = nc.sync if a < BLOCKS // 2 else nc.scalar
             store_queue.dma_start(out[a * P : (a + 1) * P, :], result[:])

import concourse.mybir as mybir
from concourse.masks import make_identity

P = 128
S = 512
M = 512
N = 384
E = 4
Q = N // E
BLOCKS = M // P
QCOLS = Q // 16
LINE = 256
WARM = 14

FLOPS = 2 * P * M * N

BF16 = mybir.dt.bfloat16
F32 = mybir.dt.float32
U16 = mybir.dt.uint16


def tile_scatter_matmul_kernel(tc, base, x, w, b, offs, out):
    nc = tc.nc
    relu = mybir.ActivationFunctionType.Relu
    add, vmax = mybir.AluOpType.add, mybir.AluOpType.max

    with (
        tc.tile_pool(name="held", bufs=1) as held,
        tc.psum_pool(name="banks", bufs=1) as banks,
    ):
        zeros_f32 = held.tile([P, P // 2], F32, name="zeros_f32")
        nc.gpsimd.memset(zeros_f32[:], 0.0)
        zeros = zeros_f32[:].bitcast(BF16)
        warm_bank = banks.tile([P, P], F32, name="warm_bank")
        for i in range(WARM):
            nc.tensor.matmul(warm_bank[:], zeros, zeros, start=True, stop=True)

        b_rows = held.tile([P, P], F32, name="b_rows")
        nc.gpsimd.memset(b_rows[:], 0.0)

        ident = held.tile([P, P], BF16, name="ident")
        make_identity(nc, ident[:])
        ident_f32 = held.tile([P, P], F32, name="ident_f32")
        make_identity(nc, ident_f32[:])

        nc.scalar.dma_start(b_rows[0:BLOCKS, :], b.rearrange("(a p) o -> a (p o)", p=P))

        early_relu = held.tile([P, 1], F32, name="early_relu")
        nc.scalar.activation(early_relu[:], zeros_f32[:, 0:1], relu)

        base_tiles = []
        for a in range(BLOCKS):
            base_tile = held.tile([P, S], BF16, name="base%d" % a, align_bytes=LINE)
            nc.sync.dma_start(base_tile[:], base[a * P : (a + 1) * P, :])
            base_tiles.append(base_tile)
        x_tile = held.tile([P, N], BF16, name="x_tile", align_bytes=LINE)
        nc.sync.dma_start(x_tile[:], x)
        offsets = held.tile([P, N // 16], U16, name="offsets")
        nc.sync.dma_start(offsets[:], offs)
        w_tiles = []
        for a in range(BLOCKS):
            w_tile = held.tile([P, E, P], BF16, name="w%d" % a, align_bytes=LINE)
            nc.sync.dma_start(w_tile[:], w[:, :, a * P : (a + 1) * P].rearrange("e k m -> k e m"))
            w_tiles.append(w_tile)

        windows = []
        for a in range(BLOCKS):
            window = banks.tile([P, S], F32, name="window%d" % a)
            nc.tensor.matmul(window[:], ident[:], base_tiles[a][:], start=True, stop=False)
            windows.append(window)

        bias_bank = banks.tile([P, P], F32, name="bias_bank")
        nc.tensor.transpose(bias_bank[:], b_rows[:], ident_f32[:])
        bias = held.tile([P, BLOCKS], F32, name="bias")
        nc.vector.tensor_copy(bias[:], bias_bank[:, 0:BLOCKS])

        for a in range(BLOCKS):
            for e in range(E):
                nc.tensor.matmul(
                    windows[a][:].indirect(offsets[:, e * QCOLS : (e + 1) * QCOLS]),
                    w_tiles[a][:, e, :],
                    x_tile[:, e * Q : (e + 1) * Q],
                    start=False,
                    stop=(e == E - 1),
                )

            result = held.tile([P, S], F32, name="result%d" % a, align_bytes=LINE)
            if a % 2 == 0:
                nc.scalar.activation(result[:], windows[a][:], relu, bias=bias[:, a : a + 1])
            else:
                nc.vector.tensor_scalar(result[:], windows[a][:], bias[:, a : a + 1], 0.0, add, vmax)
            store_queue = nc.sync if a < BLOCKS // 2 else nc.scalar
            store_queue.dma_start(out[a * P : (a + 1) * P, :], result[:])
